import numpy as np
import ml_dtypes


def mxq(x, axis, fmt="e4m3"):
    dtype, down = {"e4m3": (ml_dtypes.float8_e4m3fn, 7), "e5m2": (ml_dtypes.float8_e5m2, 14)}[fmt]
    v = np.moveaxis(np.asarray(x, np.float32).astype(ml_dtypes.bfloat16).astype(np.float64), axis, -1)
    blocks = v.reshape(v.shape[:-1] + (-1, 32))
    amax = np.abs(blocks).max(-1, keepdims=True)
    byte = np.maximum(np.where(amax > 0, np.frexp(amax)[1] - 1 + 127, 0) - down, 1)
    scale = np.exp2(byte - 127.0)
    codes = (blocks / scale).astype(np.float32).astype(dtype).astype(np.float64)
    return np.moveaxis((codes * scale).reshape(v.shape), -1, axis)


WIDE = False


def mx_kscale(k):
    if not WIDE:
        return np.ones(k)
    levels = np.array([10, -10, 5, -5, 0])
    if k % 512:
        return np.exp2(np.random.permutation(np.resize(levels, k // 32))).repeat(32)
    a = np.empty((k // 512, 16))
    for p in range(k // 512):
        a[p, :8] = np.random.permutation(np.resize(levels, 8))
        for g in range(8):
            far = levels[np.abs(levels - a[p, g]) >= 10]
            a[p, g + 8] = far[np.random.randint(len(far))]
    return np.exp2(a.ravel()).repeat(32)


def f64(x):
    return np.asarray(x).astype(np.float64)


def striped(idx):
    return np.tile(idx.reshape(-1, 16).T, (8, 1)).astype(np.uint16)


def unstriped(offs):
    return offs[:16].T.reshape(-1).astype(np.int64)


def pack_weight(w):
    k, n = w.shape
    w = f64(np.asarray(w, np.float32).astype(ml_dtypes.bfloat16)).reshape(k // 32, 32, n)
    amax = np.abs(w).max(1)
    byte = np.clip(np.where(amax > 0, np.frexp(amax)[1] - 1 + 127 - 7, 1), 1, 254)
    scaled = (w * np.exp2(127.0 - byte)[:, None, :]).reshape(k, n).astype(np.float32)
    words = np.ascontiguousarray(scaled.reshape(k // 512, 128, 4, n).transpose(0, 1, 3, 2)).astype(ml_dtypes.float8_e4m3fn).view(np.uint8)
    return words, np.ascontiguousarray(byte.astype(np.uint8).reshape(k // 512, 16, n))


def unpack_weight(words, scales):
    g, p, n, _ = words.shape
    vals = np.ascontiguousarray(words).view(ml_dtypes.float8_e4m3fn).astype(np.float64) * np.repeat(np.exp2(scales.astype(np.float64) - 127.0), 8, axis=1)[..., None]
    return vals.transpose(0, 1, 3, 2).reshape(g * 512, n)


def sigmoid(v):
    return 1.0 / (1.0 + np.exp(-np.maximum(v, -700.0)))


K, T, S, N, V = 1024, 2048, 1024, 128, 256
P = 2 ** 7


def setup_inputs():
    n = np.random.standard_normal
    s = mx_kscale(K)[:, None]
    packed_xT = pack_weight(n((K, T)) * s)
    return {
        "x_words": packed_xT[0],
        "x_scales": packed_xT[1],
        "w1": (n((K, N)) / np.sqrt(K) / s).astype(np.float32),
        "w2": (n((K, N)) / np.sqrt(K) / s).astype(np.float32),
        "gam": (np.tile(np.random.uniform(0.6, 0.95, V), (P, 1))).astype(np.float32),
        "offs": striped(np.random.permutation(T)[:S]),
        "rk1": striped(np.random.randint(0, S, V)),
        "rk2": striped(np.random.randint(0, S, V)),
        "rk3": striped(np.random.randint(0, S, V)),
        "rk4": striped(np.random.randint(0, S, V)),
    }


def reference(x_words, x_scales, w1, w2, gam, offs, rk1, rk2, rk3, rk4):
    xq = unpack_weight(x_words, x_scales)[:, unstriped(offs)]
    ya = mxq(f64(w1), 0, "e4m3").T @ xq
    att = sigmoid(ya)
    ck0 = att[:, unstriped(rk1)]
    ys = mxq(f64(w2), 0, "e4m3").T @ xq
    sat = sigmoid(ys)
    ex0 = f64(gam)[:1] * (-1.0 * (ck0 * sat[:, unstriped(rk1)]) + 1.0)
    ex1 = (f64(gam)[:1] * ex0) * (-1.0 * (att[:, unstriped(rk2)] * sat[:, unstriped(rk2)]) + 1.0)
    ex2 = (f64(gam)[:1] * ex1) * (-1.0 * (att[:, unstriped(rk3)] * sat[:, unstriped(rk3)]) + 1.0)
    ck3 = ex2 * att[:, unstriped(rk4)]
    ck1 = ex0 * att[:, unstriped(rk2)]
    ck2 = ex1 * att[:, unstriped(rk3)]
    return np.log(ck3) - (0.5 * np.log(ck1)) + ck2

@@ -1,0 +1,210 @@
+from contextlib import ExitStack
+
+import concourse.mybir as mybir
+
+F32 = mybir.dt.float32
+BF16 = mybir.dt.bfloat16
+I32 = mybir.dt.int32
+U32 = mybir.dt.uint32
+U16 = mybir.dt.uint16
+U8 = mybir.dt.uint8
+FP8X4 = mybir.dt.float8_e4m3fn_x4
+ACT = mybir.ActivationFunctionType
+ALU = mybir.AluOpType
+
+P = 128
+K, T, S, M, V = 1024, 2048, 1024, 128, 256
+PASSES = 2
+FLOPS = 2 * 2 * K * M * S
+CHUNKS = ((0, 512), (512, 768), (768, 1024))
+
+
+def tile_picked_ydbnclk_click_p_kernel(tc, x_words, x_scales, w1, w2, gam, offs, rk1, rk2, rk3, rk4, out):
+    nc = tc.nc
+    with ExitStack() as ctx:
+        keep = ctx.enter_context(tc.tile_pool(name="keep", bufs=1))
+        psum = ctx.enter_context(tc.psum_pool(name="psum", bufs=1))
+
+        def f32(name, width=V):
+            return keep.tile([P, width], F32, name=name)
+
+        planes = keep.tile([P, T], U8, name="planes", align_bytes=64)
+        nc.vector.memset(planes[:].bitcast(I32), 0)
+        warm = f32("warm", 8)
+        nc.gpsimd.memset(warm[:], 0.0)
+        warm2 = f32("warm2", 8)
+        nc.scalar.activation(warm2[:], warm[:], ACT.Sigmoid)
+
+        offs_t = keep.tile([P, S // 16], U16, name="offs_t")
+        nc.sync.dma_start(offs_t[:], offs)
+        for q in range(4):
+            nc.sync.dma_start(planes[32 * q : 32 * q + 8, :].bitcast(I32), x_scales[:, 4 * q : 4 * q + 4, :].bitcast(I32))
+        words = [keep.tile([P, T], U32, name="words%d" % o, tag="words%d" % o, align_bytes=64) for o in range(PASSES)]
+        raw = {}
+
+        def load_words(o):
+            nc.sync.dma_start(words[o][:].bitcast(I32), x_words[o].rearrange("p n t -> p (n t)").bitcast(I32))
+
+        def load_w(name, w, o):
+            raw[name, o] = keep.tile([P, 4, M], F32, name="raw_%s%d" % (name, o))
+            nc.sync.dma_start(raw[name, o][:], w[512 * o : 512 * (o + 1), :].rearrange("(p j) m -> p j m", j=4))
+
+        load_words(0)
+        for q in range(4):
+            nc.sync.dma_start(planes[32 * q : 32 * q + 8, :].bitcast(I32), x_scales[:, 4 * q : 4 * q + 4, :].bitcast(I32))
+        load_w("s", w2, 0)
+        load_w("a", w1, 0)
+        load_words(1)
+        load_w("s", w2, 1)
+        load_w("a", w1, 1)
+        ranks = []
+        for i, rk in enumerate((rk1, rk2, rk3, rk4)):
+            t = keep.tile([P, V // 16], U16, name="rk%d" % i)
+            nc.sync.dma_start(t[:], rk)
+            ranks.append(t)
+        g = f32("g")
+        nc.sync.dma_start(g[:], gam)
+
+        codes, scales, grouped = {}, {}, {}
+
+        def interleave(name, o):
+            grouped[name, o] = keep.tile([P, M, 4], BF16, name="grp_%s%d" % (name, o), tag="grp_%s%d" % (name, o), align_bytes=64)
+            nc.scalar.copy(grouped[name, o][:].rearrange("p (c i) t -> p c t i", i=4), raw[name, o][:].rearrange("p t (c i) -> p c t i", i=4))
+
+        def quantize(name, o):
+            codes[name, o] = keep.tile([P, M], U32, name="codes_%s%d" % (name, o), align_bytes=64)
+            scales[name, o] = keep.tile([P, M], U8, name="scales_%s%d" % (name, o), align_bytes=64)
+            nc.vector.quantize_mx(out=codes[name, o][:].bitcast(FP8X4), scales=scales[name, o][:], in_=grouped[name, o][:].rearrange("p m t -> p (m t)"))
+
+        picked_planes = {}
+        picked = {}
+
+        def gather_planes(c0, c1, tag=None):
+            t = keep.tile([P, c1 - c0], U8, name="planes_%d" % c0, tag=tag or "planes_%d" % c0, align_bytes=64)
+            nc.vector.tensor_copy(t[:], planes[:].indirect(offs_t[:, c0 // 16 : c1 // 16]))
+            for c in CHUNKS:
+                if c0 <= c[0] and c[1] <= c1:
+                    picked_planes[c] = (t, c[0] - c0, c[1] - c0)
+
+        def gather_words(o, c0, c1, tag=None):
+            t = keep.tile([P, c1 - c0], U32, name="picked%d_%d" % (o, c0), tag=tag or "picked%d_%d" % (o, c0), align_bytes=64)
+            nc.vector.tensor_copy(t[:], words[o][:].indirect(offs_t[:, c0 // 16 : c1 // 16]))
+            for c in CHUNKS:
+                if c0 <= c[0] and c[1] <= c1:
+                    picked[o, c] = t[:, c[0] - c0 : c[1] - c0]
+
+        acc = {}
+        for name in ("a", "s"):
+            for c in CHUNKS:
+                acc[name, c] = psum.tile([P, c[1] - c[0]], F32, name="acc_%s%d" % (name, c[0]))
+
+        def mm(name, o, c):
+            nc.tensor.matmul_mx(
+                out=acc[name, c][:],
+                lhsT=codes[name, o][:].bitcast(FP8X4),
+                lhsT_scale=scales[name, o][:],
+                rhs=picked[o, c].bitcast(FP8X4),
+                rhs_scale=picked_planes[c][0][4 * o : P, picked_planes[c][1] : picked_planes[c][2]],
+                start=(o == 0),
+                stop=(o == PASSES - 1),
+            )
+
+        ya = f32("ya", S)
+        att = f32("att", S)
+        ys = f32("ys", S)
+        sat = f32("sat", S)
+        c0, c1, c2 = CHUNKS
+        r1, r2, r3, r4 = ranks
+
+        def vg(name, win, r):
+            t = f32(name)
+            nc.vector.tensor_copy(t[:], win[:].indirect(r[:]))
+            return t
+
+        def vgm(name, win, r, other):
+            t = f32(name)
+            nc.vector.tensor_tensor(t[:], win[:].indirect(r[:]), other[:], ALU.mult)
+            return t
+
+        def sg(name, win, r):
+            t = f32(name)
+            nc.scalar.activation(t[:], win[:].indirect(r[:]), ACT.Sigmoid)
+            return t
+
+        def mul(name, a, b):
+            t = f32(name)
+            nc.vector.tensor_tensor(t[:], a[:], b[:], ALU.mult)
+            return t
+
+        def m1mul(name, a, b):
+            t = f32(name)
+            nc.vector.scalar_tensor_tensor(t[:], a[:], 1.0, b[:], ALU.subtract, ALU.mult)
+            return t
+
+        def axpy(name, a, s, b):
+            t = f32(name)
+            nc.vector.scalar_tensor_tensor(t[:], a[:], s, b[:], ALU.mult, ALU.add)
+            return t
+
+        def ln(name, a, scale):
+            t = f32(name)
+            nc.scalar.activation(t[:], a[:], ACT.Ln, scale=scale)
+            return t
+
+        def sig_out(dst, name, c):
+            nc.scalar.activation(dst[:, c[0] : c[1]], acc[name, c][:], ACT.Sigmoid)
+
+        gather_words(0, 0, S)
+        gather_planes(0, 512)
+        interleave("s", 0)
+        interleave("a", 0)
+        quantize("s", 0)
+        quantize("a", 0)
+        mm("s", 0, c0)
+        mm("a", 0, c0)
+        gather_planes(512, S, "grp_a0")
+        for c in (c1, c2):
+            mm("s", 0, c)
+            mm("a", 0, c)
+        interleave("s", 1)
+        interleave("a", 1)
+        gather_words(1, c0[0], c0[1])
+        quantize("s", 1)
+        mm("s", 1, c0)
+        gather_words(1, c1[0], c1[1], "grp_s1")
+        quantize("a", 1)
+        mm("a", 1, c0)
+        mm("s", 1, c1)
+        mm("a", 1, c1)
+        gather_words(1, c2[0], c2[1], "grp_a1")
+        mm("s", 1, c2)
+        mm("a", 1, c2)
+
+        sig_out(sat, "s", c0)
+        nc.scalar.copy(ya[:, c0[0] : c0[1]], acc["a", c0][:])
+        sig_out(sat, "s", c1)
+        sig_out(sat, "s", c2)
+        nc.vector.tensor_copy(ya[:, c1[0] : c1[1]], acc["a", c1][:])
+        nc.vector.tensor_copy(ya[:, c2[0] : c2[1]], acc["a", c2][:])
+        a2 = sg("a2", ya, r2)
+        a1 = sg("a1", ya, r1)
+        a3 = sg("a3", ya, r3)
+        a4 = sg("a4", ya, r4)
+        s1 = vg("s1", sat, r1)
+        p2 = vgm("p2", sat, r2, a2)
+        p1 = mul("p1", s1, a1)
+        u = m1mul("u", p2, g)
+        h = m1mul("h", p1, g)
+        p3 = vgm("p3", sat, r3, a3)
+        w = mul("w", h, u)
+        x = mul("x", h, a2)
+        y = m1mul("y", p3, g)
+        ck2 = mul("ck2", w, a3)
+        lx = ln("lx", x, -1.0)
+        y2 = mul("y2", y, a4)
+        z = mul("z", y2, w)
+        lz = ln("lz", z, -1.0)
+        t = axpy("t", lx, -0.5, ck2)
+        res = f32("res")
+        nc.vector.tensor_tensor(res[:], t[:], lz[:], ALU.add)
+        nc.sync.dma_start(out, res[:])

@@ -14,8 +14,13 @@ ALU = mybir.AluOpType
 
 P = 128
 K, T, S, M, V = 1024, 2048, 1024, 128, 256
-PASSES = 2
+K_PASS = 512
+PASSES = K // K_PASS
+QUADRANTS = 4
+LIST_ROWS = 16
+MX_ALIGN = 64
 FLOPS = 2 * 2 * K * M * S
+
 CHUNKS = ((0, 512), (512, 768), (768, 1024))
 
 
@@ -28,183 +33,181 @@ def tile_picked_ydbnclk_click_p_kernel(tc, x_words, x_scales, w1, w2, gam, offs,
         def f32(name, width=V):
             return keep.tile([P, width], F32, name=name)
 
-        planes = keep.tile([P, T], U8, name="planes", align_bytes=64)
+        planes = keep.tile([P, T], U8, name="planes", align_bytes=MX_ALIGN)
         nc.vector.memset(planes[:].bitcast(I32), 0)
-        warm = f32("warm", 8)
-        nc.gpsimd.memset(warm[:], 0.0)
-        warm2 = f32("warm2", 8)
-        nc.scalar.activation(warm2[:], warm[:], ACT.Sigmoid)
 
-        offs_t = keep.tile([P, S // 16], U16, name="offs_t")
+        warm_in = f32("warm_in", 8)
+        nc.gpsimd.memset(warm_in[:], 0.0)
+        warm_out = f32("warm_out", 8)
+        nc.scalar.activation(warm_out[:], warm_in[:], ACT.Sigmoid)
+
+        offs_t = keep.tile([P, S // LIST_ROWS], U16, name="offs_t")
         nc.sync.dma_start(offs_t[:], offs)
-        for q in range(4):
-            nc.sync.dma_start(planes[32 * q : 32 * q + 8, :].bitcast(I32), x_scales[:, 4 * q : 4 * q + 4, :].bitcast(I32))
-        words = [keep.tile([P, T], U32, name="words%d" % o, tag="words%d" % o, align_bytes=64) for o in range(PASSES)]
+        words = [keep.tile([P, T], U32, name="words%d" % o, align_bytes=MX_ALIGN) for o in range(PASSES)]
         raw = {}
 
         def load_words(o):
             nc.sync.dma_start(words[o][:].bitcast(I32), x_words[o].rearrange("p n t -> p (n t)").bitcast(I32))
 
-        def load_w(name, w, o):
+        def load_weights(name, w, o):
             raw[name, o] = keep.tile([P, 4, M], F32, name="raw_%s%d" % (name, o))
-            nc.sync.dma_start(raw[name, o][:], w[512 * o : 512 * (o + 1), :].rearrange("(p j) m -> p j m", j=4))
+            nc.sync.dma_start(raw[name, o][:], w[K_PASS * o : K_PASS * (o + 1), :].rearrange("(p t) m -> p t m", t=4))
 
         load_words(0)
-        for q in range(4):
-            nc.sync.dma_start(planes[32 * q : 32 * q + 8, :].bitcast(I32), x_scales[:, 4 * q : 4 * q + 4, :].bitcast(I32))
-        load_w("s", w2, 0)
-        load_w("a", w1, 0)
+        for q in range(QUADRANTS):
+            nc.sync.dma_start(planes[32 * q : 32 * q + 4 * PASSES, :].bitcast(I32), x_scales[:, 4 * q : 4 * q + 4, :].bitcast(I32))
+        load_weights("sat", w2, 0)
+        load_weights("att", w1, 0)
         load_words(1)
-        load_w("s", w2, 1)
-        load_w("a", w1, 1)
+        load_weights("sat", w2, 1)
+        load_weights("att", w1, 1)
         ranks = []
         for i, rk in enumerate((rk1, rk2, rk3, rk4)):
-            t = keep.tile([P, V // 16], U16, name="rk%d" % i)
-            nc.sync.dma_start(t[:], rk)
-            ranks.append(t)
+            ranks.append(keep.tile([P, V // LIST_ROWS], U16, name="rank%d" % (i + 1)))
+            nc.sync.dma_start(ranks[i][:], rk)
+        rank1, rank2, rank3, rank4 = ranks
         g = f32("g")
         nc.sync.dma_start(g[:], gam)
 
-        codes, scales, grouped = {}, {}, {}
+        grouped, codes, scales = {}, {}, {}
 
         def interleave(name, o):
-            grouped[name, o] = keep.tile([P, M, 4], BF16, name="grp_%s%d" % (name, o), tag="grp_%s%d" % (name, o), align_bytes=64)
-            nc.scalar.copy(grouped[name, o][:].rearrange("p (c i) t -> p c t i", i=4), raw[name, o][:].rearrange("p t (c i) -> p c t i", i=4))
+            tag = "grouped_%s%d" % (name, o)
+            grouped[name, o] = keep.tile([P, M, 4], BF16, name=tag, tag=tag, align_bytes=MX_ALIGN)
+            nc.scalar.copy(
+                grouped[name, o][:].rearrange("p (c i) t -> p c t i", i=4),
+                raw[name, o][:].rearrange("p t (c i) -> p c t i", i=4),
+            )
 
         def quantize(name, o):
-            codes[name, o] = keep.tile([P, M], U32, name="codes_%s%d" % (name, o), align_bytes=64)
-            scales[name, o] = keep.tile([P, M], U8, name="scales_%s%d" % (name, o), align_bytes=64)
-            nc.vector.quantize_mx(out=codes[name, o][:].bitcast(FP8X4), scales=scales[name, o][:], in_=grouped[name, o][:].rearrange("p m t -> p (m t)"))
+            codes[name, o] = keep.tile([P, M], U32, name="codes_%s%d" % (name, o), align_bytes=MX_ALIGN)
+            scales[name, o] = keep.tile([P, M], U8, name="scales_%s%d" % (name, o), align_bytes=MX_ALIGN)
+            nc.vector.quantize_mx(
+                out=codes[name, o][:].bitcast(FP8X4),
+                scales=scales[name, o][:],
+                in_=grouped[name, o][:].rearrange("p m t -> p (m t)"),
+            )
 
-        picked_planes = {}
-        picked = {}
+        picked_planes, picked_words = {}, {}
 
-        def gather_planes(c0, c1, tag=None):
-            t = keep.tile([P, c1 - c0], U8, name="planes_%d" % c0, tag=tag or "planes_%d" % c0, align_bytes=64)
-            nc.vector.tensor_copy(t[:], planes[:].indirect(offs_t[:, c0 // 16 : c1 // 16]))
-            for c in CHUNKS:
-                if c0 <= c[0] and c[1] <= c1:
-                    picked_planes[c] = (t, c[0] - c0, c[1] - c0)
+        def gather(source, dtype, name, lo, hi, after):
+            tag = after or name
+            tile = keep.tile([P, hi - lo], dtype, name=name, tag=tag, align_bytes=MX_ALIGN)
+            nc.vector.tensor_copy(tile[:], source[:].indirect(offs_t[:, lo // LIST_ROWS : hi // LIST_ROWS]))
+            return {c: (tile, c[0] - lo, c[1] - lo) for c in CHUNKS if lo <= c[0] and c[1] <= hi}
 
-        def gather_words(o, c0, c1, tag=None):
-            t = keep.tile([P, c1 - c0], U32, name="picked%d_%d" % (o, c0), tag=tag or "picked%d_%d" % (o, c0), align_bytes=64)
-            nc.vector.tensor_copy(t[:], words[o][:].indirect(offs_t[:, c0 // 16 : c1 // 16]))
-            for c in CHUNKS:
-                if c0 <= c[0] and c[1] <= c1:
-                    picked[o, c] = t[:, c[0] - c0 : c[1] - c0]
+        def gather_planes(lo, hi, after=None):
+            picked_planes.update(gather(planes, U8, "planes_%d" % lo, lo, hi, after))
+
+        def gather_words(o, lo, hi, after=None):
+            for c, part in gather(words[o], U32, "picked%d_%d" % (o, lo), lo, hi, after).items():
+                picked_words[o, c] = part
 
         acc = {}
-        for name in ("a", "s"):
+        for name in ("att", "sat"):
             for c in CHUNKS:
                 acc[name, c] = psum.tile([P, c[1] - c[0]], F32, name="acc_%s%d" % (name, c[0]))
 
-        def mm(name, o, c):
+        def product(name, o, c):
+            word_tile, word_lo, word_hi = picked_words[o, c]
+            plane_tile, plane_lo, plane_hi = picked_planes[c]
             nc.tensor.matmul_mx(
                 out=acc[name, c][:],
                 lhsT=codes[name, o][:].bitcast(FP8X4),
                 lhsT_scale=scales[name, o][:],
-                rhs=picked[o, c].bitcast(FP8X4),
-                rhs_scale=picked_planes[c][0][4 * o : P, picked_planes[c][1] : picked_planes[c][2]],
+                rhs=word_tile[:, word_lo:word_hi].bitcast(FP8X4),
+                rhs_scale=plane_tile[4 * o : P, plane_lo:plane_hi],
                 start=(o == 0),
                 stop=(o == PASSES - 1),
             )
 
-        ya = f32("ya", S)
-        att = f32("att", S)
-        ys = f32("ys", S)
+        att_logit = f32("att_logit", S)
         sat = f32("sat", S)
-        c0, c1, c2 = CHUNKS
-        r1, r2, r3, r4 = ranks
-
-        def vg(name, win, r):
-            t = f32(name)
-            nc.vector.tensor_copy(t[:], win[:].indirect(r[:]))
-            return t
-
-        def vgm(name, win, r, other):
-            t = f32(name)
-            nc.vector.tensor_tensor(t[:], win[:].indirect(r[:]), other[:], ALU.mult)
-            return t
-
-        def sg(name, win, r):
-            t = f32(name)
-            nc.scalar.activation(t[:], win[:].indirect(r[:]), ACT.Sigmoid)
-            return t
-
-        def mul(name, a, b):
-            t = f32(name)
-            nc.vector.tensor_tensor(t[:], a[:], b[:], ALU.mult)
-            return t
-
-        def m1mul(name, a, b):
-            t = f32(name)
-            nc.vector.scalar_tensor_tensor(t[:], a[:], 1.0, b[:], ALU.subtract, ALU.mult)
-            return t
-
-        def axpy(name, a, s, b):
-            t = f32(name)
-            nc.vector.scalar_tensor_tensor(t[:], a[:], s, b[:], ALU.mult, ALU.add)
-            return t
-
-        def ln(name, a, scale):
-            t = f32(name)
-            nc.scalar.activation(t[:], a[:], ACT.Ln, scale=scale)
-            return t
-
-        def sig_out(dst, name, c):
-            nc.scalar.activation(dst[:, c[0] : c[1]], acc[name, c][:], ACT.Sigmoid)
+        first, second, third = CHUNKS
 
         gather_words(0, 0, S)
-        gather_planes(0, 512)
-        interleave("s", 0)
-        interleave("a", 0)
-        quantize("s", 0)
-        quantize("a", 0)
-        mm("s", 0, c0)
-        mm("a", 0, c0)
-        gather_planes(512, S, "grp_a0")
-        for c in (c1, c2):
-            mm("s", 0, c)
-            mm("a", 0, c)
-        interleave("s", 1)
-        interleave("a", 1)
-        gather_words(1, c0[0], c0[1])
-        quantize("s", 1)
-        mm("s", 1, c0)
-        gather_words(1, c1[0], c1[1], "grp_s1")
-        quantize("a", 1)
-        mm("a", 1, c0)
-        mm("s", 1, c1)
-        mm("a", 1, c1)
-        gather_words(1, c2[0], c2[1], "grp_a1")
-        mm("s", 1, c2)
-        mm("a", 1, c2)
+        gather_planes(*first)
+        interleave("sat", 0)
+        interleave("att", 0)
+        quantize("sat", 0)
+        quantize("att", 0)
+        product("sat", 0, first)
+        product("att", 0, first)
+        gather_planes(second[0], S, after="grouped_att0")
+        for c in (second, third):
+            product("sat", 0, c)
+            product("att", 0, c)
 
-        sig_out(sat, "s", c0)
-        nc.scalar.copy(ya[:, c0[0] : c0[1]], acc["a", c0][:])
-        sig_out(sat, "s", c1)
-        sig_out(sat, "s", c2)
-        nc.vector.tensor_copy(ya[:, c1[0] : c1[1]], acc["a", c1][:])
-        nc.vector.tensor_copy(ya[:, c2[0] : c2[1]], acc["a", c2][:])
-        a2 = sg("a2", ya, r2)
-        a1 = sg("a1", ya, r1)
-        a3 = sg("a3", ya, r3)
-        a4 = sg("a4", ya, r4)
-        s1 = vg("s1", sat, r1)
-        p2 = vgm("p2", sat, r2, a2)
-        p1 = mul("p1", s1, a1)
-        u = m1mul("u", p2, g)
-        h = m1mul("h", p1, g)
-        p3 = vgm("p3", sat, r3, a3)
-        w = mul("w", h, u)
-        x = mul("x", h, a2)
-        y = m1mul("y", p3, g)
-        ck2 = mul("ck2", w, a3)
-        lx = ln("lx", x, -1.0)
-        y2 = mul("y2", y, a4)
-        z = mul("z", y2, w)
-        lz = ln("lz", z, -1.0)
-        t = axpy("t", lx, -0.5, ck2)
-        res = f32("res")
-        nc.vector.tensor_tensor(res[:], t[:], lz[:], ALU.add)
-        nc.sync.dma_start(out, res[:])
+        interleave("sat", 1)
+        interleave("att", 1)
+        gather_words(1, *first)
+        quantize("sat", 1)
+        product("sat", 1, first)
+        gather_words(1, *second, after="grouped_sat1")
+        quantize("att", 1)
+        product("att", 1, first)
+        product("sat", 1, second)
+        product("att", 1, second)
+        gather_words(1, *third, after="grouped_att1")
+        product("sat", 1, third)
+        product("att", 1, third)
+
+        def sigmoid_out(c):
+            nc.scalar.activation(sat[:, c[0] : c[1]], acc["sat", c][:], ACT.Sigmoid)
+
+        sigmoid_out(first)
+        nc.scalar.copy(att_logit[:, first[0] : first[1]], acc["att", first][:])
+        sigmoid_out(second)
+        sigmoid_out(third)
+        for c in (second, third):
+            nc.vector.tensor_copy(att_logit[:, c[0] : c[1]], acc["att", c][:])
+
+        def attraction(name, rank):
+            tile = f32(name)
+            nc.scalar.activation(tile[:], att_logit[:].indirect(rank[:]), ACT.Sigmoid)
+            return tile
+
+        def satisfaction_times(name, rank, other):
+            tile = f32(name)
+            nc.vector.tensor_tensor(tile[:], sat[:].indirect(rank[:]), other[:], ALU.mult)
+            return tile
+
+        def times(name, a, b):
+            tile = f32(name)
+            nc.vector.tensor_tensor(tile[:], a[:], b[:], ALU.mult)
+            return tile
+
+        def minus_go_on(name, satisfied):
+            tile = f32(name)
+            nc.vector.scalar_tensor_tensor(tile[:], satisfied[:], 1.0, g[:], ALU.subtract, ALU.mult)
+            return tile
+
+        def log_of_minus(name, a):
+            tile = f32(name)
+            nc.scalar.activation(tile[:], a[:], ACT.Ln, scale=-1.0)
+            return tile
+
+        att2 = attraction("att2", rank2)
+        att1 = attraction("att1", rank1)
+        att3 = attraction("att3", rank3)
+        att4 = attraction("att4", rank4)
+        sat1 = f32("sat1")
+        nc.vector.tensor_copy(sat1[:], sat[:].indirect(rank1[:]))
+        satisfied2 = satisfaction_times("satisfied2", rank2, att2)
+        satisfied1 = times("satisfied1", sat1, att1)
+        minus_go2 = minus_go_on("minus_go2", satisfied2)
+        minus_ex0 = minus_go_on("minus_ex0", satisfied1)
+        satisfied3 = satisfaction_times("satisfied3", rank3, att3)
+        ex1 = times("ex1", minus_ex0, minus_go2)
+        minus_ck1 = times("minus_ck1", minus_ex0, att2)
+        minus_go3 = minus_go_on("minus_go3", satisfied3)
+        ck2 = times("ck2", ex1, att3)
+        log_ck1 = log_of_minus("log_ck1", minus_ck1)
+        minus_go3_att4 = times("minus_go3_att4", minus_go3, att4)
+        minus_ck3 = times("minus_ck3", minus_go3_att4, ex1)
+        log_ck3 = log_of_minus("log_ck3", minus_ck3)
+        partial = f32("partial")
+        nc.vector.scalar_tensor_tensor(partial[:], log_ck1[:], -0.5, ck2[:], ALU.mult, ALU.add)
+        result = f32("result")
+        nc.vector.tensor_tensor(result[:], partial[:], log_ck3[:], ALU.add)
+        nc.sync.dma_start(out, result[:])

from contextlib import ExitStack

import concourse.mybir as mybir

F32 = mybir.dt.float32
BF16 = mybir.dt.bfloat16
I32 = mybir.dt.int32
U32 = mybir.dt.uint32
U16 = mybir.dt.uint16
U8 = mybir.dt.uint8
FP8X4 = mybir.dt.float8_e4m3fn_x4
ACT = mybir.ActivationFunctionType
ALU = mybir.AluOpType

P = 128
K, T, S, M, V = 1024, 2048, 1024, 128, 256
K_PASS = 512
PASSES = K // K_PASS
QUADRANTS = 4
LIST_ROWS = 16
MX_ALIGN = 64
FLOPS = 2 * 2 * K * M * S

CHUNKS = ((0, 512), (512, 768), (768, 1024))


def tile_picked_ydbnclk_click_p_kernel(tc, x_words, x_scales, w1, w2, gam, offs, rk1, rk2, rk3, rk4, out):
    nc = tc.nc
    with ExitStack() as ctx:
        keep = ctx.enter_context(tc.tile_pool(name="keep", bufs=1))
        psum = ctx.enter_context(tc.psum_pool(name="psum", bufs=1))

        def f32(name, width=V):
            return keep.tile([P, width], F32, name=name)

        planes = keep.tile([P, T], U8, name="planes", align_bytes=MX_ALIGN)
        nc.vector.memset(planes[:].bitcast(I32), 0)

        warm_in = f32("warm_in", 8)
        nc.gpsimd.memset(warm_in[:], 0.0)
        warm_out = f32("warm_out", 8)
        nc.scalar.activation(warm_out[:], warm_in[:], ACT.Sigmoid)

        offs_t = keep.tile([P, S // LIST_ROWS], U16, name="offs_t")
        nc.sync.dma_start(offs_t[:], offs)
        words = [keep.tile([P, T], U32, name="words%d" % o, align_bytes=MX_ALIGN) for o in range(PASSES)]
        raw = {}

        def load_words(o):
            nc.sync.dma_start(words[o][:].bitcast(I32), x_words[o].rearrange("p n t -> p (n t)").bitcast(I32))

        def load_weights(name, w, o):
            raw[name, o] = keep.tile([P, 4, M], F32, name="raw_%s%d" % (name, o))
            nc.sync.dma_start(raw[name, o][:], w[K_PASS * o : K_PASS * (o + 1), :].rearrange("(p t) m -> p t m", t=4))

        load_words(0)
        for q in range(QUADRANTS):
            nc.sync.dma_start(planes[32 * q : 32 * q + 4 * PASSES, :].bitcast(I32), x_scales[:, 4 * q : 4 * q + 4, :].bitcast(I32))
        load_weights("sat", w2, 0)
        load_weights("att", w1, 0)
        load_words(1)
        load_weights("sat", w2, 1)
        load_weights("att", w1, 1)
        ranks = []
        for i, rk in enumerate((rk1, rk2, rk3, rk4)):
            ranks.append(keep.tile([P, V // LIST_ROWS], U16, name="rank%d" % (i + 1)))
            nc.sync.dma_start(ranks[i][:], rk)
        rank1, rank2, rank3, rank4 = ranks
        g = f32("g")
        nc.sync.dma_start(g[:], gam)

        grouped, codes, scales = {}, {}, {}

        def interleave(name, o):
            tag = "grouped_%s%d" % (name, o)
            grouped[name, o] = keep.tile([P, M, 4], BF16, name=tag, tag=tag, align_bytes=MX_ALIGN)
            nc.scalar.copy(
                grouped[name, o][:].rearrange("p (c i) t -> p c t i", i=4),
                raw[name, o][:].rearrange("p t (c i) -> p c t i", i=4),
            )

        def quantize(name, o):
            codes[name, o] = keep.tile([P, M], U32, name="codes_%s%d" % (name, o), align_bytes=MX_ALIGN)
            scales[name, o] = keep.tile([P, M], U8, name="scales_%s%d" % (name, o), align_bytes=MX_ALIGN)
            nc.vector.quantize_mx(
                out=codes[name, o][:].bitcast(FP8X4),
                scales=scales[name, o][:],
                in_=grouped[name, o][:].rearrange("p m t -> p (m t)"),
            )

        picked_planes, picked_words = {}, {}

        def gather(source, dtype, name, lo, hi, after):
            tag = after or name
            tile = keep.tile([P, hi - lo], dtype, name=name, tag=tag, align_bytes=MX_ALIGN)
            nc.vector.tensor_copy(tile[:], source[:].indirect(offs_t[:, lo // LIST_ROWS : hi // LIST_ROWS]))
            return {c: (tile, c[0] - lo, c[1] - lo) for c in CHUNKS if lo <= c[0] and c[1] <= hi}

        def gather_planes(lo, hi, after=None):
            picked_planes.update(gather(planes, U8, "planes_%d" % lo, lo, hi, after))

        def gather_words(o, lo, hi, after=None):
            for c, part in gather(words[o], U32, "picked%d_%d" % (o, lo), lo, hi, after).items():
                picked_words[o, c] = part

        acc = {}
        for name in ("att", "sat"):
            for c in CHUNKS:
                acc[name, c] = psum.tile([P, c[1] - c[0]], F32, name="acc_%s%d" % (name, c[0]))

        def product(name, o, c):
            word_tile, word_lo, word_hi = picked_words[o, c]
            plane_tile, plane_lo, plane_hi = picked_planes[c]
            nc.tensor.matmul_mx(
                out=acc[name, c][:],
                lhsT=codes[name, o][:].bitcast(FP8X4),
                lhsT_scale=scales[name, o][:],
                rhs=word_tile[:, word_lo:word_hi].bitcast(FP8X4),
                rhs_scale=plane_tile[4 * o : P, plane_lo:plane_hi],
                start=(o == 0),
                stop=(o == PASSES - 1),
            )

        att_logit = f32("att_logit", S)
        sat = f32("sat", S)
        first, second, third = CHUNKS

        gather_words(0, 0, S)
        gather_planes(*first)
        interleave("sat", 0)
        interleave("att", 0)
        quantize("sat", 0)
        quantize("att", 0)
        product("sat", 0, first)
        product("att", 0, first)
        gather_planes(second[0], S, after="grouped_att0")
        for c in (second, third):
            product("sat", 0, c)
            product("att", 0, c)

        interleave("sat", 1)
        interleave("att", 1)
        gather_words(1, *first)
        quantize("sat", 1)
        product("sat", 1, first)
        gather_words(1, *second, after="grouped_sat1")
        quantize("att", 1)
        product("att", 1, first)
        product("sat", 1, second)
        product("att", 1, second)
        gather_words(1, *third, after="grouped_att1")
        product("sat", 1, third)
        product("att", 1, third)

        def sigmoid_out(c):
            nc.scalar.activation(sat[:, c[0] : c[1]], acc["sat", c][:], ACT.Sigmoid)

        sigmoid_out(first)
        nc.scalar.copy(att_logit[:, first[0] : first[1]], acc["att", first][:])
        sigmoid_out(second)
        sigmoid_out(third)
        for c in (second, third):
            nc.vector.tensor_copy(att_logit[:, c[0] : c[1]], acc["att", c][:])

        def attraction(name, rank):
            tile = f32(name)
            nc.scalar.activation(tile[:], att_logit[:].indirect(rank[:]), ACT.Sigmoid)
            return tile

        def satisfaction_times(name, rank, other):
            tile = f32(name)
            nc.vector.tensor_tensor(tile[:], sat[:].indirect(rank[:]), other[:], ALU.mult)
            return tile

        def times(name, a, b):
            tile = f32(name)
            nc.vector.tensor_tensor(tile[:], a[:], b[:], ALU.mult)
            return tile

        def minus_go_on(name, satisfied):
            tile = f32(name)
            nc.vector.scalar_tensor_tensor(tile[:], satisfied[:], 1.0, g[:], ALU.subtract, ALU.mult)
            return tile

        def log_of_minus(name, a):
            tile = f32(name)
            nc.scalar.activation(tile[:], a[:], ACT.Ln, scale=-1.0)
            return tile

        att2 = attraction("att2", rank2)
        att1 = attraction("att1", rank1)
        att3 = attraction("att3", rank3)
        att4 = attraction("att4", rank4)
        sat1 = f32("sat1")
        nc.vector.tensor_copy(sat1[:], sat[:].indirect(rank1[:]))
        satisfied2 = satisfaction_times("satisfied2", rank2, att2)
        satisfied1 = times("satisfied1", sat1, att1)
        minus_go2 = minus_go_on("minus_go2", satisfied2)
        minus_ex0 = minus_go_on("minus_ex0", satisfied1)
        satisfied3 = satisfaction_times("satisfied3", rank3, att3)
        ex1 = times("ex1", minus_ex0, minus_go2)
        minus_ck1 = times("minus_ck1", minus_ex0, att2)
        minus_go3 = minus_go_on("minus_go3", satisfied3)
        ck2 = times("ck2", ex1, att3)
        log_ck1 = log_of_minus("log_ck1", minus_ck1)
        minus_go3_att4 = times("minus_go3_att4", minus_go3, att4)
        minus_ck3 = times("minus_ck3", minus_go3_att4, ex1)
        log_ck3 = log_of_minus("log_ck3", minus_ck3)
        partial = f32("partial")
        nc.vector.scalar_tensor_tensor(partial[:], log_ck1[:], -0.5, ck2[:], ALU.mult, ALU.add)
        result = f32("result")
        nc.vector.tensor_tensor(result[:], partial[:], log_ck3[:], ALU.add)
        nc.sync.dma_start(out, result[:])
